import numpy as np
import ml_dtypes


def mxq(x, axis, fmt="e4m3"):
    dtype, down = {"e4m3": (ml_dtypes.float8_e4m3fn, 7), "e5m2": (ml_dtypes.float8_e5m2, 14)}[fmt]
    v = np.moveaxis(np.asarray(x, np.float32).astype(ml_dtypes.bfloat16).astype(np.float64), axis, -1)
    blocks = v.reshape(v.shape[:-1] + (-1, 32))
    amax = np.abs(blocks).max(-1, keepdims=True)
    byte = np.maximum(np.where(amax > 0, np.frexp(amax)[1] - 1 + 127, 0) - down, 1)
    scale = np.exp2(byte - 127.0)
    codes = (blocks / scale).astype(np.float32).astype(dtype).astype(np.float64)
    return np.moveaxis((codes * scale).reshape(v.shape), -1, axis)


WIDE = False


def mx_kscale(k):
    if not WIDE:
        return np.ones(k)
    levels = np.array([10, -10, 5, -5, 0])
    if k % 512:
        return np.exp2(np.random.permutation(np.resize(levels, k // 32))).repeat(32)
    a = np.empty((k // 512, 16))
    for p in range(k // 512):
        a[p, :8] = np.random.permutation(np.resize(levels, 8))
        for g in range(8):
            far = levels[np.abs(levels - a[p, g]) >= 10]
            a[p, g + 8] = far[np.random.randint(len(far))]
    return np.exp2(a.ravel()).repeat(32)


def f64(x):
    return np.asarray(x).astype(np.float64)


def striped(idx):
    return np.tile(idx.reshape(-1, 16).T, (8, 1)).astype(np.uint16)


def unstriped(offs):
    return offs[:16].T.reshape(-1).astype(np.int64)


def pack_weight(w):
    k, n = w.shape
    w = f64(np.asarray(w, np.float32).astype(ml_dtypes.bfloat16)).reshape(k // 32, 32, n)
    amax = np.abs(w).max(1)
    byte = np.clip(np.where(amax > 0, np.frexp(amax)[1] - 1 + 127 - 7, 1), 1, 254)
    scaled = (w * np.exp2(127.0 - byte)[:, None, :]).reshape(k, n).astype(np.float32)
    words = np.ascontiguousarray(scaled.reshape(k // 512, 128, 4, n).transpose(0, 1, 3, 2)).astype(ml_dtypes.float8_e4m3fn).view(np.uint8)
    return words, np.ascontiguousarray(byte.astype(np.uint8).reshape(k // 512, 16, n))


def unpack_weight(words, scales):
    g, p, n, _ = words.shape
    vals = np.ascontiguousarray(words).view(ml_dtypes.float8_e4m3fn).astype(np.float64) * np.repeat(np.exp2(scales.astype(np.float64) - 127.0), 8, axis=1)[..., None]
    return vals.transpose(0, 1, 3, 2).reshape(g * 512, n)


K, T, S, N = 1024, 1024, 512, 512


def setup_inputs():
    n = np.random.standard_normal
    s = mx_kscale(K)[:, None]
    packed = pack_weight(n((K, T)) * s)
    return {
        "x_words": packed[0],
        "x_scales": packed[1],
        "w": (n((K, N)) / np.sqrt(K) / s).astype(np.float32),
        "offs": striped(np.random.permutation(T)[:S]),
    }


def reference(x_words, x_scales, w, offs):
    idx = unstriped(offs)
    xq = unpack_weight(x_words, x_scales)[:, idx]
    y = mxq(f64(w), 0, "e4m3").T @ xq
    return y

@@ -1,0 +1,140 @@
+from contextlib import ExitStack
+
+import concourse.mybir as mybir
+
+K, T, S, N = 1024, 1024, 512, 512
+FLOPS = 2 * K * S * N
+
+F32 = mybir.dt.float32
+BF16 = mybir.dt.bfloat16
+I32 = mybir.dt.int32
+U32 = mybir.dt.uint32
+U16 = mybir.dt.uint16
+U8 = mybir.dt.uint8
+FP8X4 = mybir.dt.float8_e4m3fn_x4
+
+P = 128
+PACK = 4
+K_PASS = P * PACK
+M_TILE = 128
+
+
+def tile_picked_pick_lin_none_sub_p_kernel(tc, x_words, x_scales, w, offs, out):
+    nc = tc.nc
+    with ExitStack() as ctx:
+        keep = ctx.enter_context(tc.tile_pool(name="keep", bufs=1))
+        psum = ctx.enter_context(tc.psum_pool(name="psum", bufs=1))
+
+        offsets = keep.tile([P, S // 16], U16, name="offsets")
+        scale_window = keep.tile([P, T // 4], I32, name="scale_window", align_bytes=64)
+        word_window = [keep.tile([P, T], I32, name="word_window%d" % o, align_bytes=64) for o in range(2)]
+        x_codes = [keep.tile([P, S], U32, name="x_codes%d" % o, align_bytes=64) for o in range(2)]
+        x_scale = keep.tile([P, S], U8, name="x_scale", align_bytes=64)
+        raw, grouped, w_codes, w_scale, acc = {}, {}, {}, {}, {}
+
+        def load_words(o):
+            nc.sync.dma_start(out=word_window[o][:], in_=x_words[o].rearrange("p c r -> p (c r)").bitcast(I32))
+
+        def load_scales():
+            nc.vector.memset(scale_window[:], 0)
+            rows = x_scales.bitcast(I32)
+            for q in range(4):
+                nc.scalar.dma_start(out=scale_window[32 * q : 32 * q + 8, :], in_=rows[:, 4 * q : 4 * q + 4, :])
+
+        def load_w(o, m0, count):
+            t = keep.tile([P, PACK, count * M_TILE], F32, name="raw%d_%d" % (o, m0))
+            src = w[o * K_PASS : (o + 1) * K_PASS, m0 * M_TILE : (m0 + count) * M_TILE]
+            nc.sync.dma_start(out=t[:], in_=src.rearrange("(p j) m -> p j m", j=PACK))
+            for i in range(count):
+                raw[o, m0 + i] = t[:, :, i * M_TILE : (i + 1) * M_TILE]
+
+        def gather_words(o):
+            nc.vector.tensor_copy(out=x_codes[o][:], in_=word_window[o][:].bitcast(U32).indirect(offsets[:]))
+
+        def gather_scales():
+            nc.vector.tensor_copy(out=x_scale[:], in_=scale_window[:].bitcast(U8).indirect(offsets[:]))
+
+        def interleave(o, m, on_vector):
+            g = keep.tile([P, M_TILE, PACK], BF16, name="grouped%d_%d" % (o, m), align_bytes=64)
+            grouped[o, m] = g
+            dst = g[:].rearrange("p (c i) t -> p c t i", i=4)
+            src = raw[o, m].rearrange("p t (c i) -> p c t i", i=4)
+            if on_vector:
+                nc.vector.tensor_copy(out=dst, in_=src)
+            else:
+                nc.scalar.copy(out=dst, in_=src)
+
+        def quantize(o, m):
+            w_codes[o, m] = keep.tile([P, M_TILE], U32, name="w_codes%d_%d" % (o, m), align_bytes=64)
+            w_scale[o, m] = keep.tile([P, M_TILE], U8, name="w_scale%d_%d" % (o, m), align_bytes=64)
+            nc.vector.quantize_mx(
+                out=w_codes[o, m][:].bitcast(FP8X4),
+                scales=w_scale[o, m][:],
+                in_=grouped[o, m][:].rearrange("p c t -> p (c t)"),
+            )
+
+        def multiply(o, m, c0, width):
+            if o == 0:
+                acc[m, c0] = psum.tile([M_TILE, width], F32, name="acc%d_%d" % (m, c0))
+            nc.tensor.matmul_mx(
+                out=acc[m, c0][:],
+                lhsT=w_codes[o, m][:].bitcast(FP8X4),
+                lhsT_scale=w_scale[o, m][:],
+                rhs=x_codes[o][:, c0 : c0 + width].bitcast(FP8X4),
+                rhs_scale=x_scale[4 * o : P, c0 : c0 + width],
+                start=(o == 0),
+                stop=(o == 1),
+            )
+
+        def store(m, c0, width, on_vector):
+            res = keep.tile([M_TILE, width], F32, name="res%d_%d" % (m, c0))
+            if on_vector:
+                nc.vector.tensor_copy(out=res[:], in_=acc[m, c0][:])
+            else:
+                nc.scalar.copy(out=res[:], in_=acc[m, c0][:])
+            nc.sync.dma_start(out=out[m * M_TILE : (m + 1) * M_TILE, c0 : c0 + width], in_=res[:])
+
+        load_words(0)
+        nc.sync.dma_start(offsets[:], offs)
+        load_scales()
+        load_w(0, 0, 1)
+        load_words(1)
+        load_w(1, 0, 1)
+        load_w(0, 1, 2)
+        load_w(1, 1, 2)
+        load_w(0, 3, 1)
+        load_w(1, 3, 1)
+        gather_scales()
+        gather_words(0)
+        interleave(0, 0, False)
+        quantize(0, 0)
+        multiply(0, 0, 0, S)
+        gather_words(1)
+        interleave(1, 0, False)
+        quantize(1, 0)
+        multiply(1, 0, 0, S)
+        interleave(0, 1, True)
+        interleave(0, 2, False)
+        quantize(0, 1)
+        quantize(0, 2)
+        multiply(0, 1, 0, S)
+        multiply(0, 2, 0, S)
+        store(0, 0, S, False)
+        interleave(1, 1, True)
+        interleave(1, 2, False)
+        interleave(0, 3, True)
+        quantize(1, 1)
+        multiply(1, 1, 0, S)
+        quantize(0, 3)
+        quantize(1, 2)
+        multiply(1, 2, 0, S)
+        multiply(0, 3, 0, 256)
+        multiply(0, 3, 256, 256)
+        interleave(1, 3, True)
+        store(1, 0, S, False)
+        quantize(1, 3)
+        multiply(1, 3, 0, 256)
+        multiply(1, 3, 256, 256)
+        store(2, 0, S, False)
+        store(3, 0, 256, True)
+        store(3, 256, 256, False)

@@ -27,19 +27,25 @@ def tile_picked_pick_lin_none_sub_p_kernel(tc, x_words, x_scales, w, offs, out):
 
         offsets = keep.tile([P, S // 16], U16, name="offsets")
         scale_window = keep.tile([P, T // 4], I32, name="scale_window", align_bytes=64)
+        scale_rows = keep.tile([P, T // 4], I32, name="scale_rows", align_bytes=64)
         word_window = [keep.tile([P, T], I32, name="word_window%d" % o, align_bytes=64) for o in range(2)]
         x_codes = [keep.tile([P, S], U32, name="x_codes%d" % o, align_bytes=64) for o in range(2)]
         x_scale = keep.tile([P, S], U8, name="x_scale", align_bytes=64)
+        ring = [keep.tile([P, M_TILE, PACK], BF16, name="grouped%d" % i, align_bytes=64) for i in range(3)]
         raw, grouped, w_codes, w_scale, acc = {}, {}, {}, {}, {}
 
         def load_words(o):
             nc.sync.dma_start(out=word_window[o][:], in_=x_words[o].rearrange("p c r -> p (c r)").bitcast(I32))
 
         def load_scales():
-            nc.vector.memset(scale_window[:], 0)
             rows = x_scales.bitcast(I32)
             for q in range(4):
-                nc.scalar.dma_start(out=scale_window[32 * q : 32 * q + 8, :], in_=rows[:, 4 * q : 4 * q + 4, :])
+                nc.sync.dma_start(out=scale_rows[32 * q : 32 * q + 8, :], in_=rows[:, 4 * q : 4 * q + 4, :])
+
+        def fill_scale_window():
+            nc.vector.memset(scale_window[:], 0)
+            for q in range(4):
+                nc.vector.tensor_copy(out=scale_window[32 * q : 32 * q + 8, :], in_=scale_rows[32 * q : 32 * q + 8, :])
 
         def load_w(o, m0, count):
             t = keep.tile([P, PACK, count * M_TILE], F32, name="raw%d_%d" % (o, m0))
@@ -55,7 +61,7 @@ def tile_picked_pick_lin_none_sub_p_kernel(tc, x_words, x_scales, w, offs, out):
             nc.vector.tensor_copy(out=x_scale[:], in_=scale_window[:].bitcast(U8).indirect(offsets[:]))
 
         def interleave(o, m, on_vector):
-            g = keep.tile([P, M_TILE, PACK], BF16, name="grouped%d_%d" % (o, m), align_bytes=64)
+            g = ring[(2 * m + o) % len(ring)]
             grouped[o, m] = g
             dst = g[:].rearrange("p (c i) t -> p c t i", i=4)
             src = raw[o, m].rearrange("p t (c i) -> p c t i", i=4)
@@ -86,6 +92,18 @@ def tile_picked_pick_lin_none_sub_p_kernel(tc, x_words, x_scales, w, offs, out):
                 stop=(o == 1),
             )
 
+        def warm_up(i):
+            junk = psum.tile([M_TILE, S], F32, name="warm%d" % i)
+            nc.tensor.matmul_mx(
+                out=junk[:],
+                lhsT=x_codes[0][:, :M_TILE].bitcast(FP8X4),
+                lhsT_scale=x_scale[:, :M_TILE],
+                rhs=x_codes[0][:].bitcast(FP8X4),
+                rhs_scale=x_scale[:],
+                start=True,
+                stop=True,
+            )
+
         def store(m, c0, width, on_vector):
             res = keep.tile([M_TILE, width], F32, name="res%d_%d" % (m, c0))
             if on_vector:
@@ -94,44 +112,47 @@ def tile_picked_pick_lin_none_sub_p_kernel(tc, x_words, x_scales, w, offs, out):
                 nc.scalar.copy(out=res[:], in_=acc[m, c0][:])
             nc.sync.dma_start(out=out[m * M_TILE : (m + 1) * M_TILE, c0 : c0 + width], in_=res[:])
 
-        load_words(0)
-        nc.sync.dma_start(offsets[:], offs)
         load_scales()
-        load_w(0, 0, 1)
+        nc.sync.dma_start(offsets[:], offs)
+        load_words(0)
         load_words(1)
+        load_w(0, 0, 1)
         load_w(1, 0, 1)
-        load_w(0, 1, 2)
-        load_w(1, 1, 2)
+        load_w(0, 1, 1)
+        load_w(1, 1, 1)
+        load_w(0, 2, 1)
+        load_w(1, 2, 1)
         load_w(0, 3, 1)
         load_w(1, 3, 1)
+        fill_scale_window()
         gather_scales()
         gather_words(0)
+        gather_words(1)
         interleave(0, 0, False)
         quantize(0, 0)
         multiply(0, 0, 0, S)
-        gather_words(1)
         interleave(1, 0, False)
         quantize(1, 0)
         multiply(1, 0, 0, S)
-        interleave(0, 1, True)
-        interleave(0, 2, False)
+        interleave(0, 1, False)
         quantize(0, 1)
-        quantize(0, 2)
         multiply(0, 1, 0, S)
-        multiply(0, 2, 0, S)
-        store(0, 0, S, False)
-        interleave(1, 1, True)
-        interleave(1, 2, False)
-        interleave(0, 3, True)
+        interleave(1, 1, False)
+        interleave(0, 2, True)
         quantize(1, 1)
         multiply(1, 1, 0, S)
-        quantize(0, 3)
+        store(0, 0, S, False)
+        interleave(1, 2, True)
+        quantize(0, 2)
+        multiply(0, 2, 0, S)
+        interleave(0, 3, True)
         quantize(1, 2)
         multiply(1, 2, 0, S)
+        store(1, 0, S, False)
+        interleave(1, 3, True)
+        quantize(0, 3)
         multiply(0, 3, 0, 256)
         multiply(0, 3, 256, 256)
-        interleave(1, 3, True)
-        store(1, 0, S, False)
         quantize(1, 3)
         multiply(1, 3, 0, 256)
         multiply(1, 3, 256, 256)

@@ -17,22 +17,29 @@ P = 128
 PACK = 4
 K_PASS = P * PACK
 M_TILE = 128
+ALIGN = 256
+RAW_BYTES = PACK * M_TILE * 4
 
 
 def tile_picked_pick_lin_none_sub_p_kernel(tc, x_words, x_scales, w, offs, out):
     nc = tc.nc
     with ExitStack() as ctx:
         keep = ctx.enter_context(tc.tile_pool(name="keep", bufs=1))
+        stage = ctx.enter_context(tc.tile_pool(name="stage", bufs=1))
         psum = ctx.enter_context(tc.psum_pool(name="psum", bufs=1))
 
-        offsets = keep.tile([P, S // 16], U16, name="offsets")
-        scale_window = keep.tile([P, T // 4], I32, name="scale_window", align_bytes=64)
-        scale_rows = keep.tile([P, T // 4], I32, name="scale_rows", align_bytes=64)
-        word_window = [keep.tile([P, T], I32, name="word_window%d" % o, align_bytes=64) for o in range(2)]
-        x_codes = [keep.tile([P, S], U32, name="x_codes%d" % o, align_bytes=64) for o in range(2)]
-        x_scale = keep.tile([P, S], U8, name="x_scale", align_bytes=64)
-        ring = [keep.tile([P, M_TILE, PACK], BF16, name="grouped%d" % i, align_bytes=64) for i in range(3)]
-        raw, grouped, w_codes, w_scale, acc = {}, {}, {}, {}, {}
+        offsets = keep.tile([P, S // 16], U16, name="offsets", align_bytes=ALIGN)
+        scale_window = keep.tile([P, T // 4], I32, name="scale_window", align_bytes=ALIGN)
+        scale_rows = keep.tile([P, T // 4], I32, name="scale_rows", align_bytes=ALIGN)
+        word_window = [keep.tile([P, T], I32, name="word_window%d" % o, align_bytes=ALIGN) for o in range(2)]
+        x_scale = keep.tile([P, S], U8, name="x_scale", align_bytes=ALIGN)
+        raw, grouped, x_codes, w_codes, w_scale, acc = {}, {}, {}, {}, {}, {}
+
+        def place(shape, dtype, name, over):
+            if over is None:
+                return keep.tile(shape, dtype, name=name, align_bytes=ALIGN)
+            o, m, half = over
+            return stage.tile(shape, dtype, name=name, align_bytes=ALIGN, offset=(2 * m + o) * RAW_BYTES + half * RAW_BYTES // 2)
 
         def load_words(o):
             nc.sync.dma_start(out=word_window[o][:], in_=x_words[o].rearrange("p c r -> p (c r)").bitcast(I32))
@@ -47,32 +54,30 @@ def tile_picked_pick_lin_none_sub_p_kernel(tc, x_words, x_scales, w, offs, out):
             for q in range(4):
                 nc.vector.tensor_copy(out=scale_window[32 * q : 32 * q + 8, :], in_=scale_rows[32 * q : 32 * q + 8, :])
 
-        def load_w(o, m0, count):
-            t = keep.tile([P, PACK, count * M_TILE], F32, name="raw%d_%d" % (o, m0))
-            src = w[o * K_PASS : (o + 1) * K_PASS, m0 * M_TILE : (m0 + count) * M_TILE]
-            nc.sync.dma_start(out=t[:], in_=src.rearrange("(p j) m -> p j m", j=PACK))
-            for i in range(count):
-                raw[o, m0 + i] = t[:, :, i * M_TILE : (i + 1) * M_TILE]
+        def load_w(o, m):
+            raw[o, m] = place([P, PACK, M_TILE], F32, "raw%d_%d" % (o, m), (o, m, 0))
+            src = w[o * K_PASS : (o + 1) * K_PASS, m * M_TILE : (m + 1) * M_TILE]
+            nc.sync.dma_start(out=raw[o, m][:], in_=src.rearrange("(p j) m -> p j m", j=PACK))
 
-        def gather_words(o):
+        def gather_words(o, over=None):
+            x_codes[o] = place([P, S], U32, "x_codes%d" % o, over)
             nc.vector.tensor_copy(out=x_codes[o][:], in_=word_window[o][:].bitcast(U32).indirect(offsets[:]))
 
         def gather_scales():
             nc.vector.tensor_copy(out=x_scale[:], in_=scale_window[:].bitcast(U8).indirect(offsets[:]))
 
-        def interleave(o, m, on_vector):
-            g = ring[(2 * m + o) % len(ring)]
-            grouped[o, m] = g
-            dst = g[:].rearrange("p (c i) t -> p c t i", i=4)
-            src = raw[o, m].rearrange("p t (c i) -> p c t i", i=4)
+        def interleave(o, m, on_vector, over=None):
+            grouped[o, m] = place([P, M_TILE, PACK], BF16, "grouped%d_%d" % (o, m), over)
+            dst = grouped[o, m][:].rearrange("p (c i) t -> p c t i", i=4)
+            src = raw[o, m][:].rearrange("p t (c i) -> p c t i", i=4)
             if on_vector:
                 nc.vector.tensor_copy(out=dst, in_=src)
             else:
                 nc.scalar.copy(out=dst, in_=src)
 
-        def quantize(o, m):
-            w_codes[o, m] = keep.tile([P, M_TILE], U32, name="w_codes%d_%d" % (o, m), align_bytes=64)
-            w_scale[o, m] = keep.tile([P, M_TILE], U8, name="w_scale%d_%d" % (o, m), align_bytes=64)
+        def quantize(o, m, over=None):
+            w_codes[o, m] = place([P, M_TILE], U32, "w_codes%d_%d" % (o, m), over)
+            w_scale[o, m] = place([P, M_TILE], U8, "w_scale%d_%d" % (o, m), None)
             nc.vector.quantize_mx(
                 out=w_codes[o, m][:].bitcast(FP8X4),
                 scales=w_scale[o, m][:],
@@ -92,20 +97,8 @@ def tile_picked_pick_lin_none_sub_p_kernel(tc, x_words, x_scales, w, offs, out):
                 stop=(o == 1),
             )
 
-        def warm_up(i):
-            junk = psum.tile([M_TILE, S], F32, name="warm%d" % i)
-            nc.tensor.matmul_mx(
-                out=junk[:],
-                lhsT=x_codes[0][:, :M_TILE].bitcast(FP8X4),
-                lhsT_scale=x_scale[:, :M_TILE],
-                rhs=x_codes[0][:].bitcast(FP8X4),
-                rhs_scale=x_scale[:],
-                start=True,
-                stop=True,
-            )
-
         def store(m, c0, width, on_vector):
-            res = keep.tile([M_TILE, width], F32, name="res%d_%d" % (m, c0))
+            res = keep.tile([M_TILE, width], F32, name="res%d_%d" % (m, c0), align_bytes=ALIGN)
             if on_vector:
                 nc.vector.tensor_copy(out=res[:], in_=acc[m, c0][:])
             else:
@@ -115,38 +108,38 @@ def tile_picked_pick_lin_none_sub_p_kernel(tc, x_words, x_scales, w, offs, out):
         load_scales()
         nc.sync.dma_start(offsets[:], offs)
         load_words(0)
+        load_w(0, 0)
+        load_w(0, 1)
         load_words(1)
-        load_w(0, 0, 1)
-        load_w(1, 0, 1)
-        load_w(0, 1, 1)
-        load_w(1, 1, 1)
-        load_w(0, 2, 1)
-        load_w(1, 2, 1)
-        load_w(0, 3, 1)
-        load_w(1, 3, 1)
+        load_w(1, 0)
+        load_w(1, 1)
+        load_w(0, 2)
+        load_w(1, 2)
+        load_w(0, 3)
+        load_w(1, 3)
         fill_scale_window()
         gather_scales()
         gather_words(0)
-        gather_words(1)
         interleave(0, 0, False)
         quantize(0, 0)
         multiply(0, 0, 0, S)
-        interleave(1, 0, False)
-        quantize(1, 0)
-        multiply(1, 0, 0, S)
         interleave(0, 1, False)
         quantize(0, 1)
         multiply(0, 1, 0, S)
+        gather_words(1, (0, 1, 0))
+        interleave(1, 0, False)
+        quantize(1, 0)
+        multiply(1, 0, 0, S)
         interleave(1, 1, False)
-        interleave(0, 2, True)
         quantize(1, 1)
         multiply(1, 1, 0, S)
-        store(0, 0, S, False)
-        interleave(1, 2, True)
+        interleave(0, 2, False)
+        interleave(1, 2, True, (1, 1, 0))
         quantize(0, 2)
         multiply(0, 2, 0, S)
-        interleave(0, 3, True)
-        quantize(1, 2)
+        store(0, 0, S, False)
+        interleave(0, 3, True, (0, 2, 0))
+        quantize(1, 2, (0, 2, 1))
         multiply(1, 2, 0, S)
         store(1, 0, S, False)
         interleave(1, 3, True)

@@ -33,13 +33,14 @@ def tile_picked_pick_lin_none_sub_p_kernel(tc, x_words, x_scales, w, offs, out):
         scale_rows = keep.tile([P, T // 4], I32, name="scale_rows", align_bytes=ALIGN)
         word_window = [keep.tile([P, T], I32, name="word_window%d" % o, align_bytes=ALIGN) for o in range(2)]
         x_scale = keep.tile([P, S], U8, name="x_scale", align_bytes=ALIGN)
+        address = {}
         raw, grouped, x_codes, w_codes, w_scale, acc = {}, {}, {}, {}, {}, {}
 
         def place(shape, dtype, name, over):
             if over is None:
                 return keep.tile(shape, dtype, name=name, align_bytes=ALIGN)
-            o, m, half = over
-            return stage.tile(shape, dtype, name=name, align_bytes=ALIGN, offset=(2 * m + o) * RAW_BYTES + half * RAW_BYTES // 2)
+            chunk, start = over
+            return stage.tile(shape, dtype, name=name, align_bytes=ALIGN, offset=address[chunk] + start)
 
         def load_words(o):
             nc.sync.dma_start(out=word_window[o][:], in_=x_words[o].rearrange("p c r -> p (c r)").bitcast(I32))
@@ -54,10 +55,13 @@ def tile_picked_pick_lin_none_sub_p_kernel(tc, x_words, x_scales, w, offs, out):
             for q in range(4):
                 nc.vector.tensor_copy(out=scale_window[32 * q : 32 * q + 8, :], in_=scale_rows[32 * q : 32 * q + 8, :])
 
-        def load_w(o, m):
-            raw[o, m] = place([P, PACK, M_TILE], F32, "raw%d_%d" % (o, m), (o, m, 0))
-            src = w[o * K_PASS : (o + 1) * K_PASS, m * M_TILE : (m + 1) * M_TILE]
-            nc.sync.dma_start(out=raw[o, m][:], in_=src.rearrange("(p j) m -> p j m", j=PACK))
+        def load_w(o, m0, count=1):
+            address[o, m0] = (4 * o + m0) * RAW_BYTES
+            t = place([P, PACK, count * M_TILE], F32, "raw%d_%d" % (o, m0), ((o, m0), 0))
+            src = w[o * K_PASS : (o + 1) * K_PASS, m0 * M_TILE : (m0 + count) * M_TILE]
+            nc.sync.dma_start(out=t[:], in_=src.rearrange("(p j) m -> p j m", j=PACK))
+            for i in range(count):
+                raw[o, m0 + i] = t[:, :, i * M_TILE : (i + 1) * M_TILE]
 
         def gather_words(o, over=None):
             x_codes[o] = place([P, S], U32, "x_codes%d" % o, over)
@@ -66,10 +70,10 @@ def tile_picked_pick_lin_none_sub_p_kernel(tc, x_words, x_scales, w, offs, out):
         def gather_scales():
             nc.vector.tensor_copy(out=x_scale[:], in_=scale_window[:].bitcast(U8).indirect(offsets[:]))
 
-        def interleave(o, m, on_vector, over=None):
-            grouped[o, m] = place([P, M_TILE, PACK], BF16, "grouped%d_%d" % (o, m), over)
+        def interleave(o, m, on_vector, over=None, reuse=None):
+            grouped[o, m] = grouped[reuse] if reuse else place([P, M_TILE, PACK], BF16, "grouped%d_%d" % (o, m), over)
             dst = grouped[o, m][:].rearrange("p (c i) t -> p c t i", i=4)
-            src = raw[o, m][:].rearrange("p t (c i) -> p c t i", i=4)
+            src = raw[o, m].rearrange("p t (c i) -> p c t i", i=4)
             if on_vector:
                 nc.vector.tensor_copy(out=dst, in_=src)
             else:
@@ -108,11 +112,9 @@ def tile_picked_pick_lin_none_sub_p_kernel(tc, x_words, x_scales, w, offs, out):
         load_scales()
         nc.sync.dma_start(offsets[:], offs)
         load_words(0)
-        load_w(0, 0)
-        load_w(0, 1)
+        load_w(0, 0, 2)
         load_words(1)
-        load_w(1, 0)
-        load_w(1, 1)
+        load_w(1, 0, 2)
         load_w(0, 2)
         load_w(1, 2)
         load_w(0, 3)
@@ -126,20 +128,20 @@ def tile_picked_pick_lin_none_sub_p_kernel(tc, x_words, x_scales, w, offs, out):
         interleave(0, 1, False)
         quantize(0, 1)
         multiply(0, 1, 0, S)
-        gather_words(1, (0, 1, 0))
+        gather_words(1, ((0, 0), 0))
         interleave(1, 0, False)
+        interleave(1, 1, True, ((0, 0), 2048))
         quantize(1, 0)
         multiply(1, 0, 0, S)
-        interleave(1, 1, False)
         quantize(1, 1)
         multiply(1, 1, 0, S)
         interleave(0, 2, False)
-        interleave(1, 2, True, (1, 1, 0))
+        interleave(1, 2, True, None, (1, 0))
         quantize(0, 2)
         multiply(0, 2, 0, S)
         store(0, 0, S, False)
-        interleave(0, 3, True, (0, 2, 0))
-        quantize(1, 2, (0, 2, 1))
+        interleave(0, 3, True, ((0, 2), 0))
+        quantize(1, 2, ((0, 2), 1024))
         multiply(1, 2, 0, S)
         store(1, 0, S, False)
         interleave(1, 3, True)

@@ -30,7 +30,6 @@ def tile_picked_pick_lin_none_sub_p_kernel(tc, x_words, x_scales, w, offs, out):
 
         offsets = keep.tile([P, S // 16], U16, name="offsets", align_bytes=ALIGN)
         scale_window = keep.tile([P, T // 4], I32, name="scale_window", align_bytes=ALIGN)
-        scale_rows = keep.tile([P, T // 4], I32, name="scale_rows", align_bytes=ALIGN)
         word_window = [keep.tile([P, T], I32, name="word_window%d" % o, align_bytes=ALIGN) for o in range(2)]
         x_scale = keep.tile([P, S], U8, name="x_scale", align_bytes=ALIGN)
         address = {}
@@ -48,12 +47,7 @@ def tile_picked_pick_lin_none_sub_p_kernel(tc, x_words, x_scales, w, offs, out):
         def load_scales():
             rows = x_scales.bitcast(I32)
             for q in range(4):
-                nc.sync.dma_start(out=scale_rows[32 * q : 32 * q + 8, :], in_=rows[:, 4 * q : 4 * q + 4, :])
-
-        def fill_scale_window():
-            nc.vector.memset(scale_window[:], 0)
-            for q in range(4):
-                nc.vector.tensor_copy(out=scale_window[32 * q : 32 * q + 8, :], in_=scale_rows[32 * q : 32 * q + 8, :])
+                nc.sync.dma_start(out=scale_window[32 * q : 32 * q + 8, :], in_=rows[:, 4 * q : 4 * q + 4, :])
 
         def load_w(o, m0, count=1):
             address[o, m0] = (4 * o + m0) * RAW_BYTES
@@ -109,19 +103,20 @@ def tile_picked_pick_lin_none_sub_p_kernel(tc, x_words, x_scales, w, offs, out):
                 nc.scalar.copy(out=res[:], in_=acc[m, c0][:])
             nc.sync.dma_start(out=out[m * M_TILE : (m + 1) * M_TILE, c0 : c0 + width], in_=res[:])
 
-        load_scales()
-        nc.sync.dma_start(offsets[:], offs)
+        nc.vector.memset(scale_window[:], 0)
         load_words(0)
+        nc.sync.dma_start(offsets[:], offs)
+        load_scales()
         load_w(0, 0, 2)
         load_words(1)
-        load_w(1, 0, 2)
+        load_w(1, 0)
+        load_w(1, 1)
         load_w(0, 2)
         load_w(1, 2)
         load_w(0, 3)
         load_w(1, 3)
-        fill_scale_window()
-        gather_scales()
         gather_words(0)
+        gather_scales()
         interleave(0, 0, False)
         quantize(0, 0)
         multiply(0, 0, 0, S)
@@ -130,13 +125,13 @@ def tile_picked_pick_lin_none_sub_p_kernel(tc, x_words, x_scales, w, offs, out):
         multiply(0, 1, 0, S)
         gather_words(1, ((0, 0), 0))
         interleave(1, 0, False)
-        interleave(1, 1, True, ((0, 0), 2048))
         quantize(1, 0)
         multiply(1, 0, 0, S)
+        interleave(1, 1, False)
         quantize(1, 1)
         multiply(1, 1, 0, S)
         interleave(0, 2, False)
-        interleave(1, 2, True, None, (1, 0))
+        interleave(1, 2, True, ((1, 1), 0))
         quantize(0, 2)
         multiply(0, 2, 0, S)
         store(0, 0, S, False)

@@ -57,9 +57,15 @@ def tile_picked_pick_lin_none_sub_p_kernel(tc, x_words, x_scales, w, offs, out):
             for i in range(count):
                 raw[o, m0 + i] = t[:, :, i * M_TILE : (i + 1) * M_TILE]
 
-        def gather_words(o, over=None):
-            x_codes[o] = place([P, S], U32, "x_codes%d" % o, over)
-            nc.vector.tensor_copy(out=x_codes[o][:], in_=word_window[o][:].bitcast(U32).indirect(offsets[:]))
+        def gather_words(o, c0, width, over=None):
+            codes = place([P, width], U32, "x_codes%d_%d" % (o, c0), over)
+            entries = offsets[:, c0 // 16 : (c0 + width) // 16]
+            nc.vector.tensor_copy(out=codes[:], in_=word_window[o][:].bitcast(U32).indirect(entries))
+            x_codes[o, c0] = codes
+
+        def picked(o, c0, width):
+            first = max(c for (p, c) in x_codes if p == o and c <= c0)
+            return x_codes[o, first][:, c0 - first : c0 - first + width]
 
         def gather_scales():
             nc.vector.tensor_copy(out=x_scale[:], in_=scale_window[:].bitcast(U8).indirect(offsets[:]))
@@ -89,19 +95,22 @@ def tile_picked_pick_lin_none_sub_p_kernel(tc, x_words, x_scales, w, offs, out):
                 out=acc[m, c0][:],
                 lhsT=w_codes[o, m][:].bitcast(FP8X4),
                 lhsT_scale=w_scale[o, m][:],
-                rhs=x_codes[o][:, c0 : c0 + width].bitcast(FP8X4),
+                rhs=picked(o, c0, width).bitcast(FP8X4),
                 rhs_scale=x_scale[4 * o : P, c0 : c0 + width],
                 start=(o == 0),
                 stop=(o == 1),
             )
 
-        def store(m, c0, width, on_vector):
-            res = keep.tile([M_TILE, width], F32, name="res%d_%d" % (m, c0), align_bytes=ALIGN)
-            if on_vector:
-                nc.vector.tensor_copy(out=res[:], in_=acc[m, c0][:])
-            else:
-                nc.scalar.copy(out=res[:], in_=acc[m, c0][:])
-            nc.sync.dma_start(out=out[m * M_TILE : (m + 1) * M_TILE, c0 : c0 + width], in_=res[:])
+        def store(m, pieces):
+            first, total = pieces[0][0], sum(width for start, width, on_vector in pieces)
+            res = keep.tile([M_TILE, total], F32, name="res%d_%d" % (m, first), align_bytes=ALIGN)
+            for c0, width, on_vector in pieces:
+                dst = res[:, c0 - first : c0 - first + width]
+                if on_vector:
+                    nc.vector.tensor_copy(out=dst, in_=acc[m, c0][:])
+                else:
+                    nc.scalar.copy(out=dst, in_=acc[m, c0][:])
+            nc.sync.dma_start(out=out[m * M_TILE : (m + 1) * M_TILE, first : first + total], in_=res[:])
 
         nc.vector.memset(scale_window[:], 0)
         load_words(0)
@@ -115,30 +124,38 @@ def tile_picked_pick_lin_none_sub_p_kernel(tc, x_words, x_scales, w, offs, out):
         load_w(1, 2)
         load_w(0, 3)
         load_w(1, 3)
-        gather_words(0)
+        gather_words(0, 0, S)
         gather_scales()
         interleave(0, 0, False)
         quantize(0, 0)
-        multiply(0, 0, 0, S)
+        multiply(0, 0, 0, 256)
+        multiply(0, 0, 256, 256)
         interleave(0, 1, False)
         quantize(0, 1)
-        multiply(0, 1, 0, S)
-        gather_words(1, ((0, 0), 0))
+        multiply(0, 1, 0, 256)
+        multiply(0, 1, 256, 256)
+        gather_words(1, 0, 256, ((0, 0), 0))
         interleave(1, 0, False)
         quantize(1, 0)
-        multiply(1, 0, 0, S)
+        multiply(1, 0, 0, 256)
+        gather_words(1, 256, 256, ((1, 0), 0))
+        multiply(1, 0, 256, 256)
         interleave(1, 1, False)
         quantize(1, 1)
-        multiply(1, 1, 0, S)
+        multiply(1, 1, 0, 256)
+        multiply(1, 1, 256, 256)
         interleave(0, 2, False)
         interleave(1, 2, True, ((1, 1), 0))
         quantize(0, 2)
-        multiply(0, 2, 0, S)
-        store(0, 0, S, False)
-        interleave(0, 3, True, ((0, 2), 0))
+        multiply(0, 2, 0, 256)
+        multiply(0, 2, 256, 256)
+        store(0, [(0, 256, False)])
+        store(0, [(256, 256, False)])
         quantize(1, 2, ((0, 2), 1024))
-        multiply(1, 2, 0, S)
-        store(1, 0, S, False)
+        multiply(1, 2, 0, 256)
+        multiply(1, 2, 256, 256)
+        interleave(0, 3, True, ((0, 2), 0))
+        store(1, [(0, 256, False), (256, 256, False)])
         interleave(1, 3, True)
         quantize(0, 3)
         multiply(0, 3, 0, 256)
@@ -146,6 +163,6 @@ def tile_picked_pick_lin_none_sub_p_kernel(tc, x_words, x_scales, w, offs, out):
         quantize(1, 3)
         multiply(1, 3, 0, 256)
         multiply(1, 3, 256, 256)
-        store(2, 0, S, False)
-        store(3, 0, 256, True)
-        store(3, 256, 256, False)
+        store(2, [(0, 256, False), (256, 256, False)])
+        store(3, [(0, 256, True)])
+        store(3, [(256, 256, False)])

@@ -88,18 +88,20 @@ def tile_picked_pick_lin_none_sub_p_kernel(tc, x_words, x_scales, w, offs, out):
                 in_=grouped[o, m][:].rearrange("p c t -> p (c t)"),
             )
 
-        def multiply(o, m, c0, width):
+        def multiply(o, m, c0, width, bank=None):
             if o == 0:
-                acc[m, c0] = psum.tile([M_TILE, width], F32, name="acc%d_%d" % (m, c0))
-            nc.tensor.matmul_mx(
-                out=acc[m, c0][:],
-                lhsT=w_codes[o, m][:].bitcast(FP8X4),
-                lhsT_scale=w_scale[o, m][:],
-                rhs=picked(o, c0, width).bitcast(FP8X4),
-                rhs_scale=x_scale[4 * o : P, c0 : c0 + width],
-                start=(o == 0),
-                stop=(o == 1),
-            )
+                acc[m, c0] = psum.tile([M_TILE, width], F32, name=bank or "acc%d_%d" % (m, c0))
+            cuts = [c0] + sorted(c for (p, c) in x_codes if p == o and c0 < c < c0 + width) + [c0 + width]
+            for a, b in zip(cuts, cuts[1:]):
+                nc.tensor.matmul_mx(
+                    out=acc[m, c0][:, a - c0 : b - c0],
+                    lhsT=w_codes[o, m][:].bitcast(FP8X4),
+                    lhsT_scale=w_scale[o, m][:],
+                    rhs=picked(o, a, b - a).bitcast(FP8X4),
+                    rhs_scale=x_scale[4 * o : P, a:b],
+                    start=(o == 0),
+                    stop=(o == 1 and b == c0 + width),
+                )
 
         def store(m, pieces):
             first, total = pieces[0][0], sum(width for start, width, on_vector in pieces)
@@ -134,11 +136,11 @@ def tile_picked_pick_lin_none_sub_p_kernel(tc, x_words, x_scales, w, offs, out):
         quantize(0, 1)
         multiply(0, 1, 0, 256)
         multiply(0, 1, 256, 256)
-        gather_words(1, 0, 256, ((0, 0), 0))
+        gather_words(1, 0, 384, ((0, 0), 0))
         interleave(1, 0, False)
         quantize(1, 0)
         multiply(1, 0, 0, 256)
-        gather_words(1, 256, 256, ((1, 0), 0))
+        gather_words(1, 384, 128, ((1, 0), 0))
         multiply(1, 0, 256, 256)
         interleave(1, 1, False)
         quantize(1, 1)
@@ -158,11 +160,15 @@ def tile_picked_pick_lin_none_sub_p_kernel(tc, x_words, x_scales, w, offs, out):
         store(1, [(0, 256, False), (256, 256, False)])
         interleave(1, 3, True)
         quantize(0, 3)
-        multiply(0, 3, 0, 256)
-        multiply(0, 3, 256, 256)
+        multiply(0, 3, 0, 128)
+        multiply(0, 3, 128, 128)
         quantize(1, 3)
-        multiply(1, 3, 0, 256)
-        multiply(1, 3, 256, 256)
+        multiply(1, 3, 0, 128)
+        multiply(1, 3, 128, 128)
+        multiply(0, 3, 256, 128, "acc0_0")
+        multiply(0, 3, 384, 128, "acc0_256")
+        multiply(1, 3, 256, 128)
+        multiply(1, 3, 384, 128)
         store(2, [(0, 256, False), (256, 256, False)])
-        store(3, [(0, 256, True)])
-        store(3, [(256, 256, False)])
+        store(3, [(0, 128, True), (128, 128, False)])
+        store(3, [(256, 128, True), (384, 128, False)])

@@ -157,7 +157,8 @@ def tile_picked_pick_lin_none_sub_p_kernel(tc, x_words, x_scales, w, offs, out):
         multiply(1, 2, 0, 256)
         multiply(1, 2, 256, 256)
         interleave(0, 3, True, ((0, 2), 0))
-        store(1, [(0, 256, False), (256, 256, False)])
+        store(1, [(0, 256, False)])
+        store(1, [(256, 256, False)])
         interleave(1, 3, True)
         quantize(0, 3)
         multiply(0, 3, 0, 128)
@@ -169,6 +170,7 @@ def tile_picked_pick_lin_none_sub_p_kernel(tc, x_words, x_scales, w, offs, out):
         multiply(0, 3, 384, 128, "acc0_256")
         multiply(1, 3, 256, 128)
         multiply(1, 3, 384, 128)
-        store(2, [(0, 256, False), (256, 256, False)])
+        store(2, [(0, 256, False)])
+        store(2, [(256, 256, False)])
         store(3, [(0, 128, True), (128, 128, False)])
         store(3, [(256, 128, True), (384, 128, False)])

@@ -70,10 +70,11 @@ def tile_picked_pick_lin_none_sub_p_kernel(tc, x_words, x_scales, w, offs, out):
         def gather_scales():
             nc.vector.tensor_copy(out=x_scale[:], in_=scale_window[:].bitcast(U8).indirect(offsets[:]))
 
-        def interleave(o, m, on_vector, over=None, reuse=None):
-            grouped[o, m] = grouped[reuse] if reuse else place([P, M_TILE, PACK], BF16, "grouped%d_%d" % (o, m), over)
-            dst = grouped[o, m][:].rearrange("p (c i) t -> p c t i", i=4)
-            src = raw[o, m].rearrange("p t (c i) -> p c t i", i=4)
+        def interleave(o, m, on_vector, over=None, c0=0, c1=M_TILE):
+            if (o, m) not in grouped:
+                grouped[o, m] = place([P, M_TILE, PACK], BF16, "grouped%d_%d" % (o, m), over)
+            dst = grouped[o, m][:, c0:c1, :].rearrange("p (c i) t -> p c t i", i=4)
+            src = raw[o, m][:, :, c0:c1].rearrange("p t (c i) -> p c t i", i=4)
             if on_vector:
                 nc.vector.tensor_copy(out=dst, in_=src)
             else:
@@ -158,8 +159,9 @@ def tile_picked_pick_lin_none_sub_p_kernel(tc, x_words, x_scales, w, offs, out):
         multiply(1, 2, 256, 256)
         interleave(0, 3, True, ((0, 2), 0))
         store(1, [(0, 256, False)])
+        interleave(1, 3, False, None, 96, 128)
         store(1, [(256, 256, False)])
-        interleave(1, 3, True)
+        interleave(1, 3, True, None, 0, 96)
         quantize(0, 3)
         multiply(0, 3, 0, 128)
         multiply(0, 3, 128, 128)

@@ -33,7 +33,7 @@ def tile_picked_pick_lin_none_sub_p_kernel(tc, x_words, x_scales, w, offs, out):
         word_window = [keep.tile([P, T], I32, name="word_window%d" % o, align_bytes=ALIGN) for o in range(2)]
         x_scale = keep.tile([P, S], U8, name="x_scale", align_bytes=ALIGN)
         address = {}
-        raw, grouped, x_codes, w_codes, w_scale, acc = {}, {}, {}, {}, {}, {}
+        raw, grouped, joined, x_codes, w_codes, w_scale, acc, results = {}, {}, {}, {}, {}, {}, {}, {}
 
         def place(shape, dtype, name, over):
             if over is None:
@@ -67,46 +67,70 @@ def tile_picked_pick_lin_none_sub_p_kernel(tc, x_words, x_scales, w, offs, out):
             first = max(c for (p, c) in x_codes if p == o and c <= c0)
             return x_codes[o, first][:, c0 - first : c0 - first + width]
 
-        def gather_scales():
-            nc.vector.tensor_copy(out=x_scale[:], in_=scale_window[:].bitcast(U8).indirect(offsets[:]))
+        def gather_scales(c0=0, width=S):
+            entries = offsets[:, c0 // 16 : (c0 + width) // 16]
+            nc.vector.tensor_copy(out=x_scale[:, c0 : c0 + width], in_=scale_window[:].bitcast(U8).indirect(entries))
+
+        def warm_up(bank, width):
+            scratch = psum.tile([M_TILE, width], F32, name=bank)
+            nc.tensor.matmul_mx(
+                out=scratch[:],
+                lhsT=picked(0, 0, M_TILE).bitcast(FP8X4),
+                lhsT_scale=x_scale[:, 0:M_TILE],
+                rhs=picked(0, 0, width).bitcast(FP8X4),
+                rhs_scale=x_scale[:, 0:width],
+                start=True,
+                stop=True,
+            )
+
+        def group(o, m0, count=1, over=None):
+            t = place([P, count * M_TILE, PACK], BF16, "grouped%d_%d" % (o, m0), over)
+            joined[o, m0, count] = t
+            for i in range(count):
+                grouped[o, m0 + i] = t[:, i * M_TILE : (i + 1) * M_TILE, :]
 
         def interleave(o, m, on_vector, over=None, c0=0, c1=M_TILE):
             if (o, m) not in grouped:
-                grouped[o, m] = place([P, M_TILE, PACK], BF16, "grouped%d_%d" % (o, m), over)
-            dst = grouped[o, m][:, c0:c1, :].rearrange("p (c i) t -> p c t i", i=4)
-            src = raw[o, m][:, :, c0:c1].rearrange("p t (c i) -> p c t i", i=4)
+                group(o, m, 1, over)
+            dst = grouped[o, m][:, c0:c1, :].rearrange("p (c i) t -> p c t i", i=2)
+            src = raw[o, m][:, :, c0:c1].rearrange("p t (c i) -> p c t i", i=2)
             if on_vector:
                 nc.vector.tensor_copy(out=dst, in_=src)
             else:
                 nc.scalar.copy(out=dst, in_=src)
 
-        def quantize(o, m, over=None):
-            w_codes[o, m] = place([P, M_TILE], U32, "w_codes%d_%d" % (o, m), over)
-            w_scale[o, m] = place([P, M_TILE], U8, "w_scale%d_%d" % (o, m), None)
+        def quantize(o, m0, over=None, count=1):
+            codes = place([P, count * M_TILE], U32, "w_codes%d_%d" % (o, m0), over)
+            plane = place([P, count * M_TILE], U8, "w_scale%d_%d" % (o, m0), None)
             nc.vector.quantize_mx(
-                out=w_codes[o, m][:].bitcast(FP8X4),
-                scales=w_scale[o, m][:],
-                in_=grouped[o, m][:].rearrange("p c t -> p (c t)"),
+                out=codes[:].bitcast(FP8X4),
+                scales=plane[:],
+                in_=joined[o, m0, count][:].rearrange("p c t -> p (c t)"),
             )
+            for i in range(count):
+                w_codes[o, m0 + i] = codes[:, i * M_TILE : (i + 1) * M_TILE]
+                w_scale[o, m0 + i] = plane[:, i * M_TILE : (i + 1) * M_TILE]
 
         def multiply(o, m, c0, width, bank=None):
-            if o == 0:
+            opens = (m, c0) not in acc
+            if opens:
                 acc[m, c0] = psum.tile([M_TILE, width], F32, name=bank or "acc%d_%d" % (m, c0))
             cuts = [c0] + sorted(c for (p, c) in x_codes if p == o and c0 < c < c0 + width) + [c0 + width]
             for a, b in zip(cuts, cuts[1:]):
                 nc.tensor.matmul_mx(
                     out=acc[m, c0][:, a - c0 : b - c0],
-                    lhsT=w_codes[o, m][:].bitcast(FP8X4),
-                    lhsT_scale=w_scale[o, m][:],
+                    lhsT=w_codes[o, m].bitcast(FP8X4),
+                    lhsT_scale=w_scale[o, m],
                     rhs=picked(o, a, b - a).bitcast(FP8X4),
                     rhs_scale=x_scale[4 * o : P, a:b],
-                    start=(o == 0),
-                    stop=(o == 1 and b == c0 + width),
+                    start=opens,
+                    stop=(not opens and b == c0 + width),
                 )
 
-        def store(m, pieces):
+        def store(m, pieces, over=None):
             first, total = pieces[0][0], sum(width for start, width, on_vector in pieces)
-            res = keep.tile([M_TILE, total], F32, name="res%d_%d" % (m, first), align_bytes=ALIGN)
+            res = place([M_TILE, total], F32, "res%d_%d" % (m, first), over)
+            results[m, first] = res
             for c0, width, on_vector in pieces:
                 dst = res[:, c0 - first : c0 - first + width]
                 if on_vector:
@@ -114,6 +138,26 @@ def tile_picked_pick_lin_none_sub_p_kernel(tc, x_words, x_scales, w, offs, out):
                 else:
                     nc.scalar.copy(out=dst, in_=acc[m, c0][:])
             nc.sync.dma_start(out=out[m * M_TILE : (m + 1) * M_TILE, first : first + total], in_=res[:])
+
+        def cast_part(o, m, c0, c1, on_vector, over=None):
+            t = place([P, c1 - c0, PACK], BF16, "part%d_%d_%d" % (o, m, c0), over)
+            joined[o, m, c0, c1] = t
+            dst = t[:].rearrange("p (c i) t -> p c t i", i=2)
+            src = raw[o, m][:, :, c0:c1].rearrange("p t (c i) -> p c t i", i=2)
+            if on_vector:
+                nc.vector.tensor_copy(out=dst, in_=src)
+            else:
+                nc.scalar.copy(out=dst, in_=src)
+
+        def quantize_part(o, m, c0, c1, over=None):
+            if (o, m) not in w_codes:
+                w_codes[o, m] = place([P, M_TILE], U32, "w_codes%d_%d" % (o, m), over)[:]
+                w_scale[o, m] = place([P, M_TILE], U8, "w_scale%d_%d" % (o, m), None)[:]
+            nc.vector.quantize_mx(
+                out=w_codes[o, m][:, c0:c1].bitcast(FP8X4),
+                scales=w_scale[o, m][:, c0:c1],
+                in_=joined[o, m, c0, c1][:].rearrange("p c t -> p (c t)"),
+            )
 
         nc.vector.memset(scale_window[:], 0)
         load_words(0)

@@ -139,6 +139,11 @@ def tile_picked_pick_lin_none_sub_p_kernel(tc, x_words, x_scales, w, offs, out):
                     nc.scalar.copy(out=dst, in_=acc[m, c0][:])
             nc.sync.dma_start(out=out[m * M_TILE : (m + 1) * M_TILE, first : first + total], in_=res[:])
 
+        def store_part(m, group_start, c0, width):
+            res = place([M_TILE, width], F32, "res%d_%d" % (m, c0), None)
+            nc.scalar.copy(out=res[:], in_=acc[m, group_start][:, c0 - group_start : c0 - group_start + width])
+            nc.sync.dma_start(out=out[m * M_TILE : (m + 1) * M_TILE, c0 : c0 + width], in_=res[:])
+
         def cast_part(o, m, c0, c1, on_vector, over=None):
             t = place([P, c1 - c0, PACK], BF16, "part%d_%d_%d" % (o, m, c0), over)
             joined[o, m, c0, c1] = t
@@ -196,7 +201,8 @@ def tile_picked_pick_lin_none_sub_p_kernel(tc, x_words, x_scales, w, offs, out):
         quantize(0, 2)
         multiply(0, 2, 0, 256)
         multiply(0, 2, 256, 256)
-        store(0, [(0, 256, False)])
+        store_part(0, 0, 0, 128)
+        store_part(0, 0, 128, 128)
         store(0, [(256, 256, False)])
         quantize(1, 2, ((0, 2), 1024))
         multiply(1, 2, 0, 256)

@@ -215,14 +215,14 @@ def tile_picked_pick_lin_none_sub_p_kernel(tc, x_words, x_scales, w, offs, out):
         quantize(0, 3)
         multiply(0, 3, 0, 128)
         multiply(0, 3, 128, 128)
+        multiply(0, 3, 256, 128, "acc0_0")
+        multiply(0, 3, 384, 128, "acc0_256")
         quantize(1, 3)
         multiply(1, 3, 0, 128)
         multiply(1, 3, 128, 128)
-        multiply(0, 3, 256, 128, "acc0_0")
-        multiply(0, 3, 384, 128, "acc0_256")
         multiply(1, 3, 256, 128)
         multiply(1, 3, 384, 128)
         store(2, [(0, 256, False)])
         store(2, [(256, 256, False)])
-        store(3, [(0, 128, True), (128, 128, False)])
-        store(3, [(256, 128, True), (384, 128, False)])
+        store(3, [(0, 128, True)])
+        store(3, [(128, 128, False), (256, 128, True), (384, 128, False)])

@@ -139,11 +139,6 @@ def tile_picked_pick_lin_none_sub_p_kernel(tc, x_words, x_scales, w, offs, out):
                     nc.scalar.copy(out=dst, in_=acc[m, c0][:])
             nc.sync.dma_start(out=out[m * M_TILE : (m + 1) * M_TILE, first : first + total], in_=res[:])
 
-        def store_part(m, group_start, c0, width):
-            res = place([M_TILE, width], F32, "res%d_%d" % (m, c0), None)
-            nc.scalar.copy(out=res[:], in_=acc[m, group_start][:, c0 - group_start : c0 - group_start + width])
-            nc.sync.dma_start(out=out[m * M_TILE : (m + 1) * M_TILE, c0 : c0 + width], in_=res[:])
-
         def cast_part(o, m, c0, c1, on_vector, over=None):
             t = place([P, c1 - c0, PACK], BF16, "part%d_%d_%d" % (o, m, c0), over)
             joined[o, m, c0, c1] = t
@@ -201,8 +196,7 @@ def tile_picked_pick_lin_none_sub_p_kernel(tc, x_words, x_scales, w, offs, out):
         quantize(0, 2)
         multiply(0, 2, 0, 256)
         multiply(0, 2, 256, 256)
-        store_part(0, 0, 0, 128)
-        store_part(0, 0, 128, 128)
+        store(0, [(0, 256, False)])
         store(0, [(256, 256, False)])
         quantize(1, 2, ((0, 2), 1024))
         multiply(1, 2, 0, 256)

@@ -203,9 +203,8 @@ def tile_picked_pick_lin_none_sub_p_kernel(tc, x_words, x_scales, w, offs, out):
         multiply(1, 2, 256, 256)
         interleave(0, 3, True, ((0, 2), 0))
         store(1, [(0, 256, False)])
-        interleave(1, 3, False, None, 96, 128)
         store(1, [(256, 256, False)])
-        interleave(1, 3, True, None, 0, 96)
+        interleave(1, 3, True)
         quantize(0, 3)
         multiply(0, 3, 0, 128)
         multiply(0, 3, 128, 128)

@@ -41,8 +41,9 @@ def tile_picked_pick_lin_none_sub_p_kernel(tc, x_words, x_scales, w, offs, out):
             chunk, start = over
             return stage.tile(shape, dtype, name=name, align_bytes=ALIGN, offset=address[chunk] + start)
 
-        def load_words(o):
-            nc.sync.dma_start(out=word_window[o][:], in_=x_words[o].rearrange("p c r -> p (c r)").bitcast(I32))
+        def load_words(o, c0=0, c1=T):
+            words = x_words[o].rearrange("p c r -> p (c r)").bitcast(I32)
+            nc.sync.dma_start(out=word_window[o][:, c0:c1], in_=words[:, c0:c1])
 
         def load_scales():
             rows = x_scales.bitcast(I32)
@@ -160,7 +161,8 @@ def tile_picked_pick_lin_none_sub_p_kernel(tc, x_words, x_scales, w, offs, out):
             )
 
         nc.vector.memset(scale_window[:], 0)
-        load_words(0)
+        load_words(0, 0, T // 2)
+        load_words(0, T // 2, T)
         nc.sync.dma_start(offsets[:], offs)
         load_scales()
         load_w(0, 0, 2)

@@ -166,7 +166,8 @@ def tile_picked_pick_lin_none_sub_p_kernel(tc, x_words, x_scales, w, offs, out):
         nc.sync.dma_start(offsets[:], offs)
         load_scales()
         load_w(0, 0, 2)
-        load_words(1)
+        load_words(1, 0, T // 2)
+        load_words(1, T // 2, T)
         load_w(1, 0)
         load_w(1, 1)
         load_w(0, 2)

@@ -18,7 +18,7 @@ PACK = 4
 K_PASS = P * PACK
 M_TILE = 128
 ALIGN = 256
-RAW_BYTES = PACK * M_TILE * 4
+CHUNK_BYTES = PACK * M_TILE * 4
 
 
 def tile_picked_pick_lin_none_sub_p_kernel(tc, x_words, x_scales, w, offs, out):
@@ -32,14 +32,13 @@ def tile_picked_pick_lin_none_sub_p_kernel(tc, x_words, x_scales, w, offs, out):
         scale_window = keep.tile([P, T // 4], I32, name="scale_window", align_bytes=ALIGN)
         word_window = [keep.tile([P, T], I32, name="word_window%d" % o, align_bytes=ALIGN) for o in range(2)]
         x_scale = keep.tile([P, S], U8, name="x_scale", align_bytes=ALIGN)
-        address = {}
-        raw, grouped, joined, x_codes, w_codes, w_scale, acc, results = {}, {}, {}, {}, {}, {}, {}, {}
+        raw, rounded, x_codes, w_codes, w_scale, acc = {}, {}, {}, {}, {}, {}
 
-        def place(shape, dtype, name, over):
+        def place(shape, dtype, name, over=None):
             if over is None:
                 return keep.tile(shape, dtype, name=name, align_bytes=ALIGN)
-            chunk, start = over
-            return stage.tile(shape, dtype, name=name, align_bytes=ALIGN, offset=address[chunk] + start)
+            o, m, start = over
+            return stage.tile(shape, dtype, name=name, align_bytes=ALIGN, offset=(4 * o + m) * CHUNK_BYTES + start)
 
         def load_words(o, c0=0, c1=T):
             words = x_words[o].rearrange("p c r -> p (c r)").bitcast(I32)
@@ -51,12 +50,24 @@ def tile_picked_pick_lin_none_sub_p_kernel(tc, x_words, x_scales, w, offs, out):
                 nc.sync.dma_start(out=scale_window[32 * q : 32 * q + 8, :], in_=rows[:, 4 * q : 4 * q + 4, :])
 
         def load_w(o, m0, count=1):
-            address[o, m0] = (4 * o + m0) * RAW_BYTES
-            t = place([P, PACK, count * M_TILE], F32, "raw%d_%d" % (o, m0), ((o, m0), 0))
+            t = place([P, PACK, count * M_TILE], F32, "raw%d_%d" % (o, m0), (o, m0, 0))
             src = w[o * K_PASS : (o + 1) * K_PASS, m0 * M_TILE : (m0 + count) * M_TILE]
             nc.sync.dma_start(out=t[:], in_=src.rearrange("(p j) m -> p j m", j=PACK))
             for i in range(count):
-                raw[o, m0 + i] = t[:, :, i * M_TILE : (i + 1) * M_TILE]
+                raw[o, m0 + i, 0] = t[:, :, i * M_TILE : (i + 1) * M_TILE]
+
+        def load_w_part(o, m, c0, c1):
+            t = place([P, PACK, c1 - c0], F32, "raw%d_%d_%d" % (o, m, c0), (o, m, c0 * PACK * 4))
+            src = w[o * K_PASS : (o + 1) * K_PASS, m * M_TILE + c0 : m * M_TILE + c1]
+            nc.sync.dma_start(out=t[:], in_=src.rearrange("(p j) m -> p j m", j=PACK))
+            raw[o, m, c0] = t[:]
+
+        def load_w_rows(o, m):
+            t = place([P, PACK, M_TILE], F32, "raw%d_%d" % (o, m), (o, m, 0))
+            src = w[o * K_PASS : (o + 1) * K_PASS, m * M_TILE : (m + 1) * M_TILE].rearrange("(p j) m -> p j m", j=PACK)
+            for j in (0, 2):
+                nc.sync.dma_start(out=t[:, j : j + 2, :], in_=src[:, j : j + 2, :])
+            raw[o, m, 0] = t[:]
 
         def gather_words(o, c0, width, over=None):
             codes = place([P, width], U32, "x_codes%d_%d" % (o, c0), over)
@@ -72,45 +83,25 @@ def tile_picked_pick_lin_none_sub_p_kernel(tc, x_words, x_scales, w, offs, out):
             entries = offsets[:, c0 // 16 : (c0 + width) // 16]
             nc.vector.tensor_copy(out=x_scale[:, c0 : c0 + width], in_=scale_window[:].bitcast(U8).indirect(entries))
 
-        def warm_up(bank, width):
-            scratch = psum.tile([M_TILE, width], F32, name=bank)
-            nc.tensor.matmul_mx(
-                out=scratch[:],
-                lhsT=picked(0, 0, M_TILE).bitcast(FP8X4),
-                lhsT_scale=x_scale[:, 0:M_TILE],
-                rhs=picked(0, 0, width).bitcast(FP8X4),
-                rhs_scale=x_scale[:, 0:width],
-                start=True,
-                stop=True,
-            )
-
-        def group(o, m0, count=1, over=None):
-            t = place([P, count * M_TILE, PACK], BF16, "grouped%d_%d" % (o, m0), over)
-            joined[o, m0, count] = t
-            for i in range(count):
-                grouped[o, m0 + i] = t[:, i * M_TILE : (i + 1) * M_TILE, :]
-
-        def interleave(o, m, on_vector, over=None, c0=0, c1=M_TILE):
-            if (o, m) not in grouped:
-                group(o, m, 1, over)
-            dst = grouped[o, m][:, c0:c1, :].rearrange("p (c i) t -> p c t i", i=2)
-            src = raw[o, m][:, :, c0:c1].rearrange("p t (c i) -> p c t i", i=2)
-            if on_vector:
+        def cast(o, m, engine, over=None, c0=0, c1=M_TILE):
+            if (o, m) not in rounded:
+                rounded[o, m] = place([P, M_TILE, PACK], BF16, "rounded%d_%d" % (o, m), over)
+            dst = rounded[o, m][:, c0:c1, :].rearrange("p (c i) t -> p c t i", i=2)
+            first = max(c for (p, n, c) in raw if (p, n) == (o, m) and c <= c0)
+            src = raw[o, m, first][:, :, c0 - first : c1 - first].rearrange("p t (c i) -> p c t i", i=2)
+            if engine == "vector":
                 nc.vector.tensor_copy(out=dst, in_=src)
             else:
                 nc.scalar.copy(out=dst, in_=src)
 
-        def quantize(o, m0, over=None, count=1):
-            codes = place([P, count * M_TILE], U32, "w_codes%d_%d" % (o, m0), over)
-            plane = place([P, count * M_TILE], U8, "w_scale%d_%d" % (o, m0), None)
+        def quantize(o, m, over=None):
+            w_codes[o, m] = place([P, M_TILE], U32, "w_codes%d_%d" % (o, m), over)
+            w_scale[o, m] = place([P, M_TILE], U8, "w_scale%d_%d" % (o, m))
             nc.vector.quantize_mx(
-                out=codes[:].bitcast(FP8X4),
-                scales=plane[:],
-                in_=joined[o, m0, count][:].rearrange("p c t -> p (c t)"),
+                out=w_codes[o, m][:].bitcast(FP8X4),
+                scales=w_scale[o, m][:],
+                in_=rounded[o, m][:].rearrange("p c t -> p (c t)"),
             )
-            for i in range(count):
-                w_codes[o, m0 + i] = codes[:, i * M_TILE : (i + 1) * M_TILE]
-                w_scale[o, m0 + i] = plane[:, i * M_TILE : (i + 1) * M_TILE]
 
         def multiply(o, m, c0, width, bank=None):
             opens = (m, c0) not in acc
@@ -120,8 +111,8 @@ def tile_picked_pick_lin_none_sub_p_kernel(tc, x_words, x_scales, w, offs, out):
             for a, b in zip(cuts, cuts[1:]):
                 nc.tensor.matmul_mx(
                     out=acc[m, c0][:, a - c0 : b - c0],
-                    lhsT=w_codes[o, m].bitcast(FP8X4),
-                    lhsT_scale=w_scale[o, m],
+                    lhsT=w_codes[o, m][:].bitcast(FP8X4),
+                    lhsT_scale=w_scale[o, m][:],
                     rhs=picked(o, a, b - a).bitcast(FP8X4),
                     rhs_scale=x_scale[4 * o : P, a:b],
                     start=opens,
@@ -129,45 +120,25 @@ def tile_picked_pick_lin_none_sub_p_kernel(tc, x_words, x_scales, w, offs, out):
                 )
 
         def store(m, pieces, over=None):
-            first, total = pieces[0][0], sum(width for start, width, on_vector in pieces)
+            first, total = pieces[0][0], sum(width for start, width, engine in pieces)
             res = place([M_TILE, total], F32, "res%d_%d" % (m, first), over)
-            results[m, first] = res
-            for c0, width, on_vector in pieces:
+            for c0, width, engine in pieces:
                 dst = res[:, c0 - first : c0 - first + width]
-                if on_vector:
+                if engine == "vector":
                     nc.vector.tensor_copy(out=dst, in_=acc[m, c0][:])
                 else:
                     nc.scalar.copy(out=dst, in_=acc[m, c0][:])
             nc.sync.dma_start(out=out[m * M_TILE : (m + 1) * M_TILE, first : first + total], in_=res[:])
 
-        def cast_part(o, m, c0, c1, on_vector, over=None):
-            t = place([P, c1 - c0, PACK], BF16, "part%d_%d_%d" % (o, m, c0), over)
-            joined[o, m, c0, c1] = t
-            dst = t[:].rearrange("p (c i) t -> p c t i", i=2)
-            src = raw[o, m][:, :, c0:c1].rearrange("p t (c i) -> p c t i", i=2)
-            if on_vector:
-                nc.vector.tensor_copy(out=dst, in_=src)
-            else:
-                nc.scalar.copy(out=dst, in_=src)
-
-        def quantize_part(o, m, c0, c1, over=None):
-            if (o, m) not in w_codes:
-                w_codes[o, m] = place([P, M_TILE], U32, "w_codes%d_%d" % (o, m), over)[:]
-                w_scale[o, m] = place([P, M_TILE], U8, "w_scale%d_%d" % (o, m), None)[:]
-            nc.vector.quantize_mx(
-                out=w_codes[o, m][:, c0:c1].bitcast(FP8X4),
-                scales=w_scale[o, m][:, c0:c1],
-                in_=joined[o, m, c0, c1][:].rearrange("p c t -> p (c t)"),
-            )
-
+        V, A = "vector", "scalar"
         nc.vector.memset(scale_window[:], 0)
-        load_words(0, 0, T // 2)
-        load_words(0, T // 2, T)
+        load_words(0, 0, 256)
+        load_words(0, 256, T)
         nc.sync.dma_start(offsets[:], offs)
         load_scales()
         load_w(0, 0, 2)
-        load_words(1, 0, T // 2)
-        load_words(1, T // 2, T)
+        load_words(1, 0, 768)
+        load_words(1, 768, T)
         load_w(1, 0)
         load_w(1, 1)
         load_w(0, 2)
@@ -176,38 +147,38 @@ def tile_picked_pick_lin_none_sub_p_kernel(tc, x_words, x_scales, w, offs, out):
         load_w(1, 3)
         gather_words(0, 0, S)
         gather_scales()
-        interleave(0, 0, False)
+        cast(0, 0, A)
         quantize(0, 0)
         multiply(0, 0, 0, 256)
         multiply(0, 0, 256, 256)
-        interleave(0, 1, False)
+        cast(0, 1, A)
         quantize(0, 1)
         multiply(0, 1, 0, 256)
         multiply(0, 1, 256, 256)
-        gather_words(1, 0, 384, ((0, 0), 0))
-        interleave(1, 0, False)
+        gather_words(1, 0, 384, (0, 0, 0))
+        cast(1, 0, A)
         quantize(1, 0)
         multiply(1, 0, 0, 256)
-        gather_words(1, 384, 128, ((1, 0), 0))
+        gather_words(1, 384, 128, (1, 0, 0))
         multiply(1, 0, 256, 256)
-        interleave(1, 1, False)
+        cast(1, 1, A)
         quantize(1, 1)
         multiply(1, 1, 0, 256)
         multiply(1, 1, 256, 256)
-        interleave(0, 2, False)
-        interleave(1, 2, True, ((1, 1), 0))
+        cast(0, 2, A)
+        cast(1, 2, V, (1, 1, 0))
         quantize(0, 2)
         multiply(0, 2, 0, 256)
         multiply(0, 2, 256, 256)
-        store(0, [(0, 256, False)])
-        store(0, [(256, 256, False)])
-        quantize(1, 2, ((0, 2), 1024))
+        store(0, [(0, 256, A)])
+        store(0, [(256, 256, A)])
+        quantize(1, 2, (0, 2, 1024))
         multiply(1, 2, 0, 256)
         multiply(1, 2, 256, 256)
-        interleave(0, 3, True, ((0, 2), 0))
-        store(1, [(0, 256, False)])
-        store(1, [(256, 256, False)])
-        interleave(1, 3, True)
+        cast(0, 3, V, (0, 2, 0))
+        store(1, [(0, 256, A)])
+        store(1, [(256, 256, A)])
+        cast(1, 3, V)
         quantize(0, 3)
         multiply(0, 3, 0, 128)
         multiply(0, 3, 128, 128)
@@ -218,7 +189,7 @@ def tile_picked_pick_lin_none_sub_p_kernel(tc, x_words, x_scales, w, offs, out):
         multiply(1, 3, 128, 128)
         multiply(1, 3, 256, 128)
         multiply(1, 3, 384, 128)
-        store(2, [(0, 256, False)])
-        store(2, [(256, 256, False)])
-        store(3, [(0, 128, True)])
-        store(3, [(128, 128, False), (256, 128, True), (384, 128, False)])
+        store(2, [(0, 256, A)])
+        store(2, [(256, 256, A)])
+        store(3, [(0, 128, V)])
+        store(3, [(128, 128, A), (256, 128, V), (384, 128, A)])

from contextlib import ExitStack

import concourse.mybir as mybir

K, T, S, N = 1024, 1024, 512, 512
FLOPS = 2 * K * S * N

F32 = mybir.dt.float32
BF16 = mybir.dt.bfloat16
I32 = mybir.dt.int32
U32 = mybir.dt.uint32
U16 = mybir.dt.uint16
U8 = mybir.dt.uint8
FP8X4 = mybir.dt.float8_e4m3fn_x4

P = 128
PACK = 4
K_PASS = P * PACK
M_TILE = 128
ALIGN = 256
CHUNK_BYTES = PACK * M_TILE * 4


def tile_picked_pick_lin_none_sub_p_kernel(tc, x_words, x_scales, w, offs, out):
    nc = tc.nc
    with ExitStack() as ctx:
        keep = ctx.enter_context(tc.tile_pool(name="keep", bufs=1))
        stage = ctx.enter_context(tc.tile_pool(name="stage", bufs=1))
        psum = ctx.enter_context(tc.psum_pool(name="psum", bufs=1))

        offsets = keep.tile([P, S // 16], U16, name="offsets", align_bytes=ALIGN)
        scale_window = keep.tile([P, T // 4], I32, name="scale_window", align_bytes=ALIGN)
        word_window = [keep.tile([P, T], I32, name="word_window%d" % o, align_bytes=ALIGN) for o in range(2)]
        x_scale = keep.tile([P, S], U8, name="x_scale", align_bytes=ALIGN)
        raw, rounded, x_codes, w_codes, w_scale, acc = {}, {}, {}, {}, {}, {}

        def place(shape, dtype, name, over=None):
            if over is None:
                return keep.tile(shape, dtype, name=name, align_bytes=ALIGN)
            o, m, start = over
            return stage.tile(shape, dtype, name=name, align_bytes=ALIGN, offset=(4 * o + m) * CHUNK_BYTES + start)

        def load_words(o, c0=0, c1=T):
            words = x_words[o].rearrange("p c r -> p (c r)").bitcast(I32)
            nc.sync.dma_start(out=word_window[o][:, c0:c1], in_=words[:, c0:c1])

        def load_scales():
            rows = x_scales.bitcast(I32)
            for q in range(4):
                nc.sync.dma_start(out=scale_window[32 * q : 32 * q + 8, :], in_=rows[:, 4 * q : 4 * q + 4, :])

        def load_w(o, m0, count=1):
            t = place([P, PACK, count * M_TILE], F32, "raw%d_%d" % (o, m0), (o, m0, 0))
            src = w[o * K_PASS : (o + 1) * K_PASS, m0 * M_TILE : (m0 + count) * M_TILE]
            nc.sync.dma_start(out=t[:], in_=src.rearrange("(p j) m -> p j m", j=PACK))
            for i in range(count):
                raw[o, m0 + i, 0] = t[:, :, i * M_TILE : (i + 1) * M_TILE]

        def load_w_part(o, m, c0, c1):
            t = place([P, PACK, c1 - c0], F32, "raw%d_%d_%d" % (o, m, c0), (o, m, c0 * PACK * 4))
            src = w[o * K_PASS : (o + 1) * K_PASS, m * M_TILE + c0 : m * M_TILE + c1]
            nc.sync.dma_start(out=t[:], in_=src.rearrange("(p j) m -> p j m", j=PACK))
            raw[o, m, c0] = t[:]

        def load_w_rows(o, m):
            t = place([P, PACK, M_TILE], F32, "raw%d_%d" % (o, m), (o, m, 0))
            src = w[o * K_PASS : (o + 1) * K_PASS, m * M_TILE : (m + 1) * M_TILE].rearrange("(p j) m -> p j m", j=PACK)
            for j in (0, 2):
                nc.sync.dma_start(out=t[:, j : j + 2, :], in_=src[:, j : j + 2, :])
            raw[o, m, 0] = t[:]

        def gather_words(o, c0, width, over=None):
            codes = place([P, width], U32, "x_codes%d_%d" % (o, c0), over)
            entries = offsets[:, c0 // 16 : (c0 + width) // 16]
            nc.vector.tensor_copy(out=codes[:], in_=word_window[o][:].bitcast(U32).indirect(entries))
            x_codes[o, c0] = codes

        def picked(o, c0, width):
            first = max(c for (p, c) in x_codes if p == o and c <= c0)
            return x_codes[o, first][:, c0 - first : c0 - first + width]

        def gather_scales(c0=0, width=S):
            entries = offsets[:, c0 // 16 : (c0 + width) // 16]
            nc.vector.tensor_copy(out=x_scale[:, c0 : c0 + width], in_=scale_window[:].bitcast(U8).indirect(entries))

        def cast(o, m, engine, over=None, c0=0, c1=M_TILE):
            if (o, m) not in rounded:
                rounded[o, m] = place([P, M_TILE, PACK], BF16, "rounded%d_%d" % (o, m), over)
            dst = rounded[o, m][:, c0:c1, :].rearrange("p (c i) t -> p c t i", i=2)
            first = max(c for (p, n, c) in raw if (p, n) == (o, m) and c <= c0)
            src = raw[o, m, first][:, :, c0 - first : c1 - first].rearrange("p t (c i) -> p c t i", i=2)
            if engine == "vector":
                nc.vector.tensor_copy(out=dst, in_=src)
            else:
                nc.scalar.copy(out=dst, in_=src)

        def quantize(o, m, over=None):
            w_codes[o, m] = place([P, M_TILE], U32, "w_codes%d_%d" % (o, m), over)
            w_scale[o, m] = place([P, M_TILE], U8, "w_scale%d_%d" % (o, m))
            nc.vector.quantize_mx(
                out=w_codes[o, m][:].bitcast(FP8X4),
                scales=w_scale[o, m][:],
                in_=rounded[o, m][:].rearrange("p c t -> p (c t)"),
            )

        def multiply(o, m, c0, width, bank=None):
            opens = (m, c0) not in acc
            if opens:
                acc[m, c0] = psum.tile([M_TILE, width], F32, name=bank or "acc%d_%d" % (m, c0))
            cuts = [c0] + sorted(c for (p, c) in x_codes if p == o and c0 < c < c0 + width) + [c0 + width]
            for a, b in zip(cuts, cuts[1:]):
                nc.tensor.matmul_mx(
                    out=acc[m, c0][:, a - c0 : b - c0],
                    lhsT=w_codes[o, m][:].bitcast(FP8X4),
                    lhsT_scale=w_scale[o, m][:],
                    rhs=picked(o, a, b - a).bitcast(FP8X4),
                    rhs_scale=x_scale[4 * o : P, a:b],
                    start=opens,
                    stop=(not opens and b == c0 + width),
                )

        def store(m, pieces, over=None):
            first, total = pieces[0][0], sum(width for start, width, engine in pieces)
            res = place([M_TILE, total], F32, "res%d_%d" % (m, first), over)
            for c0, width, engine in pieces:
                dst = res[:, c0 - first : c0 - first + width]
                if engine == "vector":
                    nc.vector.tensor_copy(out=dst, in_=acc[m, c0][:])
                else:
                    nc.scalar.copy(out=dst, in_=acc[m, c0][:])
            nc.sync.dma_start(out=out[m * M_TILE : (m + 1) * M_TILE, first : first + total], in_=res[:])

        V, A = "vector", "scalar"
        nc.vector.memset(scale_window[:], 0)
        load_words(0, 0, 256)
        load_words(0, 256, T)
        nc.sync.dma_start(offsets[:], offs)
        load_scales()
        load_w(0, 0, 2)
        load_words(1, 0, 768)
        load_words(1, 768, T)
        load_w(1, 0)
        load_w(1, 1)
        load_w(0, 2)
        load_w(1, 2)
        load_w(0, 3)
        load_w(1, 3)
        gather_words(0, 0, S)
        gather_scales()
        cast(0, 0, A)
        quantize(0, 0)
        multiply(0, 0, 0, 256)
        multiply(0, 0, 256, 256)
        cast(0, 1, A)
        quantize(0, 1)
        multiply(0, 1, 0, 256)
        multiply(0, 1, 256, 256)
        gather_words(1, 0, 384, (0, 0, 0))
        cast(1, 0, A)
        quantize(1, 0)
        multiply(1, 0, 0, 256)
        gather_words(1, 384, 128, (1, 0, 0))
        multiply(1, 0, 256, 256)
        cast(1, 1, A)
        quantize(1, 1)
        multiply(1, 1, 0, 256)
        multiply(1, 1, 256, 256)
        cast(0, 2, A)
        cast(1, 2, V, (1, 1, 0))
        quantize(0, 2)
        multiply(0, 2, 0, 256)
        multiply(0, 2, 256, 256)
        store(0, [(0, 256, A)])
        store(0, [(256, 256, A)])
        quantize(1, 2, (0, 2, 1024))
        multiply(1, 2, 0, 256)
        multiply(1, 2, 256, 256)
        cast(0, 3, V, (0, 2, 0))
        store(1, [(0, 256, A)])
        store(1, [(256, 256, A)])
        cast(1, 3, V)
        quantize(0, 3)
        multiply(0, 3, 0, 128)
        multiply(0, 3, 128, 128)
        multiply(0, 3, 256, 128, "acc0_0")
        multiply(0, 3, 384, 128, "acc0_256")
        quantize(1, 3)
        multiply(1, 3, 0, 128)
        multiply(1, 3, 128, 128)
        multiply(1, 3, 256, 128)
        multiply(1, 3, 384, 128)
        store(2, [(0, 256, A)])
        store(2, [(256, 256, A)])
        store(3, [(0, 128, V)])
        store(3, [(128, 128, A), (256, 128, V), (384, 128, A)])
